import numpy as np
import ml_dtypes


def mxq(x, axis, fmt="e4m3"):
    dtype, down = {"e4m3": (ml_dtypes.float8_e4m3fn, 7), "e5m2": (ml_dtypes.float8_e5m2, 14)}[fmt]
    v = np.moveaxis(np.asarray(x, np.float32).astype(ml_dtypes.bfloat16).astype(np.float64), axis, -1)
    blocks = v.reshape(v.shape[:-1] + (-1, 32))
    amax = np.abs(blocks).max(-1, keepdims=True)
    byte = np.maximum(np.where(amax > 0, np.frexp(amax)[1] - 1 + 127, 0) - down, 1)
    scale = np.exp2(byte - 127.0)
    codes = (blocks / scale).astype(np.float32).astype(dtype).astype(np.float64)
    return np.moveaxis((codes * scale).reshape(v.shape), -1, axis)


WIDE = False


def mx_kscale(k):
    if not WIDE:
        return np.ones(k)
    levels = np.array([10, -10, 5, -5, 0])
    if k % 512:
        return np.exp2(np.random.permutation(np.resize(levels, k // 32))).repeat(32)
    a = np.empty((k // 512, 16))
    for p in range(k // 512):
        a[p, :8] = np.random.permutation(np.resize(levels, 8))
        for g in range(8):
            far = levels[np.abs(levels - a[p, g]) >= 10]
            a[p, g + 8] = far[np.random.randint(len(far))]
    return np.exp2(a.ravel()).repeat(32)


def f64(x):
    return np.asarray(x).astype(np.float64)


def striped(idx):
    return np.tile(idx.reshape(-1, 16).T, (8, 1)).astype(np.uint16)


def unstriped(offs):
    return offs[:16].T.reshape(-1).astype(np.int64)


def striped8(idx):
    return np.concatenate([x.reshape(-1, 16).T for x in idx]).astype(np.uint16)


def runs(offs, k):
    lists = np.stack([offs[16 * r : 16 * r + 16].T.reshape(-1) for r in range(8)]).astype(np.int64)
    return lists[np.arange(k) % 512 // 64]


def pack_weight(w):
    k, n = w.shape
    w = f64(np.asarray(w, np.float32).astype(ml_dtypes.bfloat16)).reshape(k // 32, 32, n)
    amax = np.abs(w).max(1)
    byte = np.clip(np.where(amax > 0, np.frexp(amax)[1] - 1 + 127 - 7, 1), 1, 254)
    scaled = (w * np.exp2(127.0 - byte)[:, None, :]).reshape(k, n).astype(np.float32)
    words = np.ascontiguousarray(scaled.reshape(k // 512, 128, 4, n).transpose(0, 1, 3, 2)).astype(ml_dtypes.float8_e4m3fn).view(np.uint8)
    return words, np.ascontiguousarray(byte.astype(np.uint8).reshape(k // 512, 16, n))


def unpack_weight(words, scales):
    g, p, n, _ = words.shape
    vals = np.ascontiguousarray(words).view(ml_dtypes.float8_e4m3fn).astype(np.float64) * np.repeat(np.exp2(scales.astype(np.float64) - 127.0), 8, axis=1)[..., None]
    return vals.transpose(0, 1, 3, 2).reshape(g * 512, n)


def sigmoid(v):
    return 1.0 / (1.0 + np.exp(-np.maximum(v, -700.0)))

def planes(y):
    n, m = y.shape
    v = y.astype(np.float32).astype(ml_dtypes.bfloat16).astype(np.float64).reshape(n // 32, 32, m)
    top = np.abs(v).max(1)
    byte = np.clip(np.where(top > 0, np.frexp(top)[1] - 1 + 127 - 7, 1), 1, 254)
    codes = (v * np.exp2(127.0 - byte)[:, None, :]).reshape(n, m).astype(np.float32).astype(ml_dtypes.float8_e4m3fn).view(np.uint8)
    words = codes.reshape(n // 512, 128, 4, m).transpose(0, 1, 3, 2)
    return np.ascontiguousarray(words), np.ascontiguousarray(byte.astype(np.uint8).reshape(n // 512, 16, m))


K, T, S, V, H = 512, 2048, 512, 512, 512


def setup_inputs():
    n = np.random.standard_normal
    s = mx_kscale(K)[:, None]
    u = mx_kscale(S)
    packed_xT = pack_weight(n((K, T)) * s)
    packed_w1 = pack_weight(n((K, H)) / np.sqrt(K) / s)
    packed_w2 = pack_weight(n((K, H)) / np.sqrt(K) / s)
    return {
        "x_words": packed_xT[0],
        "x_scales": packed_xT[1],
        "w1_words": packed_w1[0],
        "w1_scales": packed_w1[1],
        "w2_words": packed_w2[0],
        "w2_scales": packed_w2[1],
        "ga": (np.random.uniform(0.5, 1.5, (H, 1)) * u[:, None]).astype(np.float32),
        "gb": (np.random.uniform(0.5, 1.5, (H, 1)) / u[:, None]).astype(np.float32),
        "offs": striped(np.random.permutation(T)[:S]),
        "two": striped(np.random.permutation(T)[:V]),
        "n1": striped8(np.stack([np.random.permutation(S) for _ in range(8)])),
        "n2": striped8(np.stack([np.random.permutation(S) for _ in range(8)])),
        "n3": striped8(np.stack([np.random.permutation(S) for _ in range(8)])),
        "n4": striped8(np.stack([np.random.permutation(S) for _ in range(8)])),
        "n5": striped8(np.stack([np.random.permutation(V) for _ in range(8)])),
        "n6": striped8(np.stack([np.random.permutation(V) for _ in range(8)])),
        "n7": striped8(np.stack([np.random.permutation(V) for _ in range(8)])),
        "n8": striped8(np.stack([np.random.permutation(V) for _ in range(8)])),
        "n9": striped8(np.stack([np.random.permutation(V) for _ in range(8)])),
        "n10": striped8(np.stack([np.random.permutation(V) for _ in range(8)])),
    }


def reference(x_words, x_scales, w1_words, w1_scales, w2_words, w2_scales, ga, gb, offs, two, n1, n2, n3, n4, n5, n6, n7, n8, n9, n10):
    xq = unpack_weight(x_words, x_scales)[:, unstriped(offs)]
    a = unpack_weight(w1_words, w1_scales).T @ xq
    z = f64(ga) * (0.75 * ((a[np.arange(H)[:, None], runs(n1, H)]) * (a[np.arange(H)[:, None], runs(n2, H)]) - ((a[np.arange(H)[:, None], runs(n3, H)]) * (a[np.arange(H)[:, None], runs(n4, H)]))))
    x_two = unpack_weight(x_words, x_scales)[:, unstriped(two)]
    b = unpack_weight(w2_words, w2_scales).T @ x_two
    z2 = f64(gb) * ((b[np.arange(H)[:, None], runs(n5, H)]) * sigmoid(b) + (b[np.arange(H)[:, None], runs(n6, H)]) * (sigmoid(b[np.arange(H)[:, None], runs(n7, H)])))
    s = 0.0625 * ((mxq(z, 0, "e4m3").T @ mxq(z2, 0, "e4m3")))
    b1 = s[np.arange(S)[:, None], runs(n8, S)]
    b2 = s[np.arange(S)[:, None], runs(n9, S)]
    b3 = s[np.arange(S)[:, None], runs(n10, S)]
    out_0 = np.maximum(np.maximum(b1, b2), b3) - (0.5 * (np.maximum(np.minimum(b1, b2), np.minimum(np.maximum(b1, b2), b3))))
    return (out_0,) + planes(out_0)

@@ -1,0 +1,273 @@
+from contextlib import ExitStack
+
+import concourse.mybir as mybir
+from concourse.masks import make_identity
+
+K, T, S, V, H = 512, 2048, 512, 512, 512
+FLOPS = 2 * K * H * S + 2 * K * H * V + 2 * H * S * V
+
+F32 = mybir.dt.float32
+BF16 = mybir.dt.bfloat16
+I32 = mybir.dt.int32
+U32 = mybir.dt.uint32
+U16 = mybir.dt.uint16
+U8 = mybir.dt.uint8
+FP8X4 = mybir.dt.float8_e4m3fn_x4
+ALU = mybir.AluOpType
+ACT = mybir.ActivationFunctionType
+
+P = 128
+PACK = 4
+B_PIECES = [(0, 256), (256, 128), (384, 128)]
+TURNED = 2
+G_BUFS = 2
+
+
+def tile_picked_kqdetwsumtop2_none_po_kernel(
+    tc, x_words, x_scales, w1_words, w1_scales, w2_words, w2_scales, ga, gb,
+    offs, two, n1, n2, n3, n4, n5, n6, n7, n8, n9, n10, out_0, out_1, out_2,
+):
+    nc = tc.nc
+    with ExitStack() as ctx:
+        held = ctx.enter_context(tc.tile_pool(name="held", bufs=1))
+        work = ctx.enter_context(tc.tile_pool(name="work", bufs=2))
+        psum = ctx.enter_context(tc.psum_pool(name="psum", bufs=8))
+
+        def load_list(name, src):
+            tile = held.tile([P, 32], U16, name=name)
+            nc.sync.dma_start(tile[:], src)
+            return tile
+
+        def entries(lst, c0, n):
+            return lst[:, c0 // 16 : (c0 + n) // 16]
+
+        def words_of(dram):
+            return dram[0].rearrange("p n t -> p (n t)").bitcast(I32)
+
+        def load_scale_rows(tile, first, dram, queues):
+            rows = dram[0].bitcast(I32)
+            for q in range(4):
+                queues[q].dma_start(tile[32 * q + first : 32 * q + first + 4, :].bitcast(I32), rows[4 * q : 4 * q + 4, :])
+
+        xs = held.tile([P, T], U8, name="xs", align_bytes=64)
+        ws_raw = held.tile([P, H], U8, name="ws_raw", tag="ws_raw", align_bytes=64)
+        nc.gpsimd.memset(xs[:].bitcast(I32), 0)
+        nc.gpsimd.memset(ws_raw[:].bitcast(I32), 0)
+
+        warm = held.tile([P, 2], F32, name="warm")
+        nc.vector.memset(warm[:, 0:1], 0.0)
+        nc.scalar.activation(warm[:, 1:2], warm[:, 0:1], ACT.Sigmoid)
+
+
+        def add_turned(dst, terms):
+            for i, term in enumerate(terms):
+                nc.tensor.matmul(dst, lhsT=term, rhs=ident[:], is_transpose=True, start=(i == 0), stop=(i == len(terms) - 1))
+
+        def turn_back_pairs(bank, back, c0):
+            turned = work.tile([P, PACK * P], BF16, name="turned")
+            nc.scalar.copy(turned[:].rearrange("j (u p e) -> j u p e", u=2, e=2), bank[:].rearrange("j (u e p) -> j u p e", u=2, e=2))
+            words = turned[:].bitcast(F32)
+            for u in range(2):
+                nc.tensor.transpose(back[:, u * 256 + c0 : u * 256 + c0 + P], words[:, u * P : (u + 1) * P], ident[:])
+
+        w1_raw = held.tile([P, H], I32, name="w1_raw")
+        w2_raw = held.tile([P, H], I32, name="w2_raw")
+        xw = held.tile([P, T], I32, name="xw", align_bytes=64)
+        ga_t = held.tile([P, PACK], F32, name="ga_t")
+        gb_t = held.tile([P, PACK], F32, name="gb_t")
+        load_scale_rows(xs, 0, x_scales, [nc.sync] * 4)
+        l_offs = load_list("l_offs", offs)
+        l_two = load_list("l_two", two)
+        nc.sync.dma_start(w1_raw[:], words_of(w1_words))
+        nc.sync.dma_start(xw[:], words_of(x_words))
+        load_scale_rows(ws_raw, 0, w1_scales, [nc.sync] * 4)
+        load_scale_rows(ws_raw, 4, w2_scales, [nc.sync, nc.sync, nc.gpsimd, nc.gpsimd])
+        l1 = load_list("l1", n1)
+        nc.sync.dma_start(ga_t[:], ga.rearrange("(p t) o -> p (t o)", t=PACK))
+        l3 = load_list("l3", n3)
+        l2 = load_list("l2", n2)
+        nc.sync.dma_start(w2_raw[:], words_of(w2_words))
+        l4 = load_list("l4", n4)
+        nc.sync.dma_start(gb_t[:], gb.rearrange("(p t) o -> p (t o)", t=PACK))
+        l7 = load_list("l7", n7)
+        l5 = load_list("l5", n5)
+        l6 = load_list("l6", n6)
+        l8 = load_list("l8", n8)
+        l9 = load_list("l9", n9)
+        l10 = load_list("l10", n10)
+
+        ident = held.tile([P, P], F32, name="ident")
+        make_identity(nc, ident[:])
+
+        def deal(dst, src):
+            nc.vector.tensor_copy(dst[:].rearrange("p (t m) -> p m t", t=PACK), src[:].rearrange("p (m t) -> p m t", t=PACK))
+
+        w1 = held.tile([P, H], I32, name="w1", align_bytes=64)
+        w2 = held.tile([P, H], I32, name="w2", align_bytes=64)
+        ws = held.tile([P, H], U8, name="ws", align_bytes=64)
+
+        def pick(window, lst, dtype, name, tag=None):
+            picked = held.tile([P, S], dtype, name=name, tag=tag or name, align_bytes=64)
+            nc.vector.tensor_copy(picked[:], window.indirect(lst[:]))
+            return picked
+
+        xa_s = pick(xs[:], l_offs, U8, "xa_s")
+        xb_s = pick(xs[:], l_two, U8, "xb_s")
+        deal(w1, w1_raw)
+        xa_w = pick(xw[:].bitcast(U32), l_offs, U32, "xa_w")
+        deal(ws, ws_raw)
+
+        def project(w, first, words, scales, t):
+            bank = psum.tile([P, 512], F32, name="bank")
+            cols = slice(t * P, (t + 1) * P)
+            nc.tensor.matmul_mx(
+                bank[:], lhsT=w[:, cols].bitcast(FP8X4), lhsT_scale=ws[first:P, cols],
+                rhs=words[:].bitcast(FP8X4), rhs_scale=scales[:], start=True, stop=True,
+            )
+            return bank
+
+        a_win, ca_win = [], []
+        for t in range(PACK):
+            bank = project(w1, 0, xa_w, xa_s, t)
+            a_t = held.tile([P, 2 * S], F32, name="a%d" % t)
+            ca_t = held.tile([P, 2 * S], F32, name="ca%d" % t)
+            nc.scalar.copy(a_t[:, 0:S], bank[:])
+            nc.scalar.activation(ca_t[:, 0:S], bank[:], ACT.Copy, scale=ga_t[:, t : t + 1])
+            a_win.append(a_t)
+            ca_win.append(ca_t)
+
+        xb_w = pick(xw[:].bitcast(U32), l_two, U32, "xb_w", "ws_raw")
+        deal(w2, w2_raw)
+
+        gb_win, sig, sig7 = [], [], []
+        for t in range(PACK):
+            bank = project(w2, 4, xb_w, xb_s, t)
+            b_t = held.tile([P, 2 * V], F32, name="b%d" % t)
+            gb_b = held.tile([P, 2 * V], F32, name="gbb%d" % t)
+            sig_t = held.tile([P, V], F32, name="sig%d" % t)
+            sig7_t = held.tile([P, V], F32, name="sigg%d" % t)
+            nc.scalar.copy(b_t[:, 0:V], bank[:])
+            nc.scalar.activation(gb_b[:, 0:V], bank[:], ACT.Copy, scale=gb_t[:, t : t + 1])
+            nc.scalar.activation(sig_t[:], bank[:], ACT.Sigmoid)
+            nc.scalar.activation(sig7_t[:], b_t[:].indirect(l7[:]), ACT.Sigmoid)
+            gb_win.append(gb_b)
+            sig.append(sig_t)
+            sig7.append(sig7_t)
+
+        z_banks = [psum.tile([P, 512], F32, name="bank") for jb in range(4)]
+        for t in range(PACK):
+            g1 = work.tile([P, S], F32, name="g1")
+            g3 = work.tile([P, S], F32, name="g3")
+            p12 = work.tile([P, S], F32, name="p12")
+            p34 = work.tile([P, S], F32, name="p34")
+            nc.vector.tensor_scalar(g1[:], a_win[t][:].indirect(l1[:]), 0.75, 0.0, ALU.mult, ALU.add)
+            nc.vector.tensor_scalar(g3[:], a_win[t][:].indirect(l3[:]), -0.75, 0.0, ALU.mult, ALU.add)
+            nc.vector.tensor_tensor(p12[:], ca_win[t][:].indirect(l2[:]), g1[:], ALU.mult)
+            nc.vector.tensor_tensor(p34[:], ca_win[t][:].indirect(l4[:]), g3[:], ALU.mult)
+            for jb in range(4):
+                cols = slice(jb * P, (jb + 1) * P)
+                add_turned(z_banks[jb][:, t * P : (t + 1) * P], [p12[:, cols], p34[:, cols]])
+        z_bf = held.tile([P, S * PACK], BF16, name="z_bf", align_bytes=64)
+        z_pairs = z_bf[:].bitcast(F32).rearrange("p (r m u) -> p r m u", r=PACK, u=2)
+        for h in range(2):
+            back = psum.tile([P, 512], F32, name="bank")
+            for i in range(2):
+                turn_back_pairs(z_banks[2 * h + i], back, i * P)
+            nc.scalar.copy(z_pairs[:, :, 64 * h : 64 * h + 64, :], back[:].rearrange("p (u m r) -> p r m u", u=2, r=PACK))
+        z_w = held.tile([P, S], U32, name="z_w", align_bytes=64)
+        z_s = held.tile([P, S], U8, name="z_s", align_bytes=64)
+
+        def interleave(engine_copy, dst, src):
+            engine_copy(
+                dst[:].rearrange("p (c i t) -> p c t i", i=4, t=PACK),
+                src.rearrange("p t (c i) -> p c t i", i=4),
+            )
+
+        nc.vector.quantize_mx(z_w[:].bitcast(FP8X4), z_s[:], z_bf[:])
+
+        z2 = held.tile([P, PACK, V], F32, name="z2")
+        early = held.tile([P, 6 * V], F32, name="early")
+        late = z_bf[:].bitcast(F32)
+        s_win = [held.tile([P, 2 * V], F32, name="s%d" % t) for t in range(PACK)]
+
+        def gated(t, c0, n):
+            pair = early[:, 2 * V * t : 2 * V * (t + 1)] if t < PACK - 1 else late
+            p5_t = pair[:, c0 : c0 + n]
+            p6_t = pair[:, V + c0 : V + c0 + n]
+            nc.vector.tensor_tensor(p5_t, gb_win[t][:].indirect(entries(l5, c0, n)), sig[t][:, c0 : c0 + n], ALU.mult)
+            nc.vector.tensor_tensor(p6_t, gb_win[t][:].indirect(entries(l6, c0, n)), sig7[t][:, c0 : c0 + n], ALU.mult)
+            nc.vector.tensor_tensor(z2[:, t, c0 : c0 + n], p5_t, p6_t, ALU.add)
+
+        for t in range(PACK - 1):
+            gated(t, 0, V)
+        quantised = []
+        for ci, (c0, n) in enumerate(B_PIECES):
+            gated(PACK - 1, c0, n)
+            z2_bf = held.tile([P, n * PACK], BF16, name="z2_bf%d" % ci, align_bytes=64)
+            interleave(nc.vector.tensor_copy if ci == len(B_PIECES) - 1 else nc.scalar.copy, z2_bf, z2[:, :, c0 : c0 + n])
+            z2_w = held.tile([P, n], U32, name="z2_w%d" % ci, align_bytes=64)
+            z2_s = held.tile([P, n], U8, name="z2_s%d" % ci, align_bytes=64)
+            nc.vector.quantize_mx(z2_w[:].bitcast(FP8X4), z2_s[:], z2_bf[:])
+            quantised.append((z2_w, z2_s))
+        last0 = B_PIECES[-1][0]
+        for t in range(PACK):
+            cols = slice(t * P, (t + 1) * P)
+            banks = [psum.tile([P, 512], F32, name="bank") for i in range(2)]
+            for (c0, n), (z2_w, z2_s) in zip(B_PIECES, quantised):
+                nc.tensor.matmul_mx(
+                    banks[c0 // last0][:, c0 : c0 + n], lhsT=z_w[:, cols].bitcast(FP8X4), lhsT_scale=z_s[:, cols],
+                    rhs=z2_w[:].bitcast(FP8X4), rhs_scale=z2_s[:], start=True, stop=True,
+                )
+            nc.scalar.activation(s_win[t][:, 0:last0], banks[0][:, 0:last0], ACT.Copy, scale=0.03125)
+            nc.scalar.activation(s_win[t][:, last0:V], banks[1][:, last0:V], ACT.Copy, scale=0.03125)
+
+        out_rows = out_0.rearrange("(p t) v -> p t v", t=PACK)
+        out_words = words_of(out_1)
+        out_scales = out_2[0].bitcast(I32)
+        y = held.tile([P, PACK, V], F32, name="y")
+        y_w = held.tile([P, V], I32, name="y_w", align_bytes=64)
+        y_s = held.tile([P, V], U8, name="y_s", align_bytes=64)
+        for t in range(PACK):
+            b1 = work.tile([P, V], F32, name="b1", bufs=G_BUFS)
+            d = work.tile([P, V], F32, name="d")
+            hi = work.tile([P, V], F32, name="hi")
+            ad = work.tile([P, V], F32, name="ad")
+            f = work.tile([P, V], F32, name="f")
+            wv = work.tile([P, V], F32, name="wv")
+            xv = work.tile([P, V], F32, name="xv")
+            pieces = [(0, V)] if t < PACK - 1 else [(0, 256), (256, 256)]
+            for c0, n in pieces:
+                c = slice(c0, c0 + n)
+                nc.vector.tensor_copy(b1[:, c], s_win[t][:].indirect(entries(l8, c0, n)))
+                nc.vector.tensor_tensor(d[:, c], s_win[t][:].indirect(entries(l9, c0, n)), b1[:, c], ALU.subtract)
+                nc.vector.scalar_tensor_tensor(hi[:, c], d[:, c], 0.0, b1[:, c], ALU.max, ALU.add)
+                nc.scalar.activation(ad[:, c], d[:, c], ACT.Abs)
+                nc.vector.tensor_tensor(f[:, c], s_win[t][:].indirect(entries(l10, c0, n)), hi[:, c], ALU.subtract)
+                nc.vector.scalar_tensor_tensor(wv[:, c], f[:, c], -1.0, ad[:, c], ALU.mult, ALU.min)
+                if t < TURNED:
+                    rw = work.tile([P, V], F32, name="rw")
+                    nc.scalar.activation(xv[:], f[:], ACT.Relu, scale=2.0)
+                    nc.scalar.activation(rw[:], wv[:], ACT.Relu)
+                    bank = psum.tile([P, 512], F32, name="bank")
+                    for i in range(V // P):
+                        cols = slice(i * P, (i + 1) * P)
+                        add_turned(bank[:, cols], [hi[:, cols], xv[:, cols], rw[:, cols]])
+                    y_turned = work.tile([P, 512], F32, name="y_turned")
+                    nc.scalar.copy(y_turned[:], bank[:])
+                    back = psum.tile([P, 512], F32, name="bank")
+                    for i in range(V // P):
+                        cols = slice(i * P, (i + 1) * P)
+                        nc.tensor.transpose(back[:, cols], y_turned[:, cols], ident[:])
+                    nc.scalar.copy(y[:, t, :], back[:])
+                else:
+                    nc.vector.scalar_tensor_tensor(xv[:, c], f[:, c], 2.0, wv[:, c], ALU.mult, ALU.max)
+                    nc.vector.tensor_tensor(y[:, t, c], hi[:, c], xv[:, c], ALU.add)
+                nc.sync.dma_start(out_rows[:, t, c], y[:, t, c])
+                if t == PACK - 1:
+                    y_bf = held.tile([P, n * PACK], BF16, name="y_bf%d" % c0, align_bytes=64)
+                    interleave(nc.vector.tensor_copy if c0 else nc.scalar.copy, y_bf, y[:, :, c])
+                    nc.vector.quantize_mx(y_w[:, c].bitcast(FP8X4), y_s[:, c], y_bf[:])
+                    nc.sync.dma_start(out_words[:, c], y_w[:, c])
+        for q in range(4):
+            (nc.sync if q % 2 else nc.scalar).dma_start(
+                out_scales[4 * q : 4 * q + 4, :], y_s[32 * q : 32 * q + 4, :].bitcast(I32))

@@ -17,10 +17,14 @@ ALU = mybir.AluOpType
 ACT = mybir.ActivationFunctionType
 
 P = 128
-PACK = 4
-B_PIECES = [(0, 256), (256, 128), (384, 128)]
-TURNED = 2
-G_BUFS = 2
+QUARTERS = 4
+N = 512
+RUN = 8
+BLOCKS = [slice(c, c + P) for c in range(0, N, P)]
+HALF = N // 2
+HALVES = [slice(0, HALF), slice(HALF, N)]
+WHOLE = slice(0, N)
+LAST = QUARTERS - 1
 
 
 def tile_picked_kqdetwsumtop2_none_po_kernel(
@@ -31,64 +35,67 @@ def tile_picked_kqdetwsumtop2_none_po_kernel(
     with ExitStack() as ctx:
         held = ctx.enter_context(tc.tile_pool(name="held", bufs=1))
         work = ctx.enter_context(tc.tile_pool(name="work", bufs=2))
-        psum = ctx.enter_context(tc.psum_pool(name="psum", bufs=8))
+        psum = ctx.enter_context(tc.psum_pool(name="psum", bufs=2))
 
-        def load_list(name, src):
-            tile = held.tile([P, 32], U16, name=name)
-            nc.sync.dma_start(tile[:], src)
-            return tile
+        def bank(tag):
+            return psum.tile([P, N], F32, name=tag, bufs=4 if tag == "backs" else 2)
 
-        def entries(lst, c0, n):
-            return lst[:, c0 // 16 : (c0 + n) // 16]
+        def sum_bank(piece):
+            return bank("sums" if piece < 2 else "late_sums")
+
+        def window(name, tag=None):
+            return held.tile([P, 2 * N], F32, name=name, tag=tag or name)
+
+        def look_up(tile, entries, cols):
+            return tile[:].indirect(entries[:, cols.start // 16 : cols.stop // 16])
 
         def words_of(dram):
             return dram[0].rearrange("p n t -> p (n t)").bitcast(I32)
 
-        def load_scale_rows(tile, first, dram, queues):
-            rows = dram[0].bitcast(I32)
-            for q in range(4):
-                queues[q].dma_start(tile[32 * q + first : 32 * q + first + 4, :].bitcast(I32), rows[4 * q : 4 * q + 4, :])
-
-        xs = held.tile([P, T], U8, name="xs", align_bytes=64)
-        ws_raw = held.tile([P, H], U8, name="ws_raw", tag="ws_raw", align_bytes=64)
-        nc.gpsimd.memset(xs[:].bitcast(I32), 0)
-        nc.gpsimd.memset(ws_raw[:].bitcast(I32), 0)
+        x_scale = held.tile([P, T], U8, name="x_scale", align_bytes=64)
+        w1_scale_in = held.tile([P, H], U8, name="w1_scale_in", tag="w1_scale_in", align_bytes=64)
+        w2_scale_in = held.tile([P, H], U8, name="w2_scale_in", align_bytes=64)
+        gain_rows = held.tile([P, P], F32, name="gain_rows")
+        for tile in (x_scale, w1_scale_in, w2_scale_in):
+            nc.gpsimd.memset(tile[:].bitcast(I32), 0)
+        nc.gpsimd.memset(gain_rows[:], 0.0)
+        ident = held.tile([P, P], F32, name="ident")
+        make_identity(nc, ident[:])
 
         warm = held.tile([P, 2], F32, name="warm")
         nc.vector.memset(warm[:, 0:1], 0.0)
         nc.scalar.activation(warm[:, 1:2], warm[:, 0:1], ACT.Sigmoid)
 
+        def load_list(name, dram):
+            tile = held.tile([P, N // 16], U16, name=name)
+            nc.sync.dma_start(tile[:], dram)
+            return tile
 
-        def add_turned(dst, terms):
-            for i, term in enumerate(terms):
-                nc.tensor.matmul(dst, lhsT=term, rhs=ident[:], is_transpose=True, start=(i == 0), stop=(i == len(terms) - 1))
+        def load_scales(tile, dram):
+            rows = dram[0].bitcast(I32)
+            for q in range(4):
+                nc.sync.dma_start(tile[32 * q : 32 * q + 4, :].bitcast(I32), rows[4 * q : 4 * q + 4, :])
 
-        def turn_back_pairs(bank, back, c0):
-            turned = work.tile([P, PACK * P], BF16, name="turned")
-            nc.scalar.copy(turned[:].rearrange("j (u p e) -> j u p e", u=2, e=2), bank[:].rearrange("j (u e p) -> j u p e", u=2, e=2))
-            words = turned[:].bitcast(F32)
-            for u in range(2):
-                nc.tensor.transpose(back[:, u * 256 + c0 : u * 256 + c0 + P], words[:, u * P : (u + 1) * P], ident[:])
-
-        w1_raw = held.tile([P, H], I32, name="w1_raw")
-        w2_raw = held.tile([P, H], I32, name="w2_raw")
-        xw = held.tile([P, T], I32, name="xw", align_bytes=64)
-        ga_t = held.tile([P, PACK], F32, name="ga_t")
-        gb_t = held.tile([P, PACK], F32, name="gb_t")
-        load_scale_rows(xs, 0, x_scales, [nc.sync] * 4)
+        x_word = held.tile([P, T], I32, name="x_word", align_bytes=64)
+        w1_in = held.tile([P, H], I32, name="w1_in")
+        w2_in = held.tile([P, H], I32, name="w2_in")
+        load_scales(x_scale, x_scales)
         l_offs = load_list("l_offs", offs)
         l_two = load_list("l_two", two)
-        nc.sync.dma_start(w1_raw[:], words_of(w1_words))
-        nc.sync.dma_start(xw[:], words_of(x_words))
-        load_scale_rows(ws_raw, 0, w1_scales, [nc.sync] * 4)
-        load_scale_rows(ws_raw, 4, w2_scales, [nc.sync, nc.sync, nc.gpsimd, nc.gpsimd])
+        nc.sync.dma_start(x_word[:], words_of(x_words))
+        nc.sync.dma_start(w1_in[:], words_of(w1_words))
+        load_scales(w1_scale_in, w1_scales)
         l1 = load_list("l1", n1)
-        nc.sync.dma_start(ga_t[:], ga.rearrange("(p t) o -> p (t o)", t=PACK))
         l3 = load_list("l3", n3)
+        nc.sync.dma_start(w2_in[:], words_of(w2_words))
+        load_scales(w2_scale_in, w2_scales)
+        for first, gain in ((0, ga), (QUARTERS, gb)):
+            nc.sync.dma_start(
+                gain_rows[first : first + QUARTERS, :].rearrange("t (g r) -> t g r", r=RUN),
+                gain.rearrange("(g t r) o -> t g (r o)", t=QUARTERS, r=RUN),
+            )
         l2 = load_list("l2", n2)
-        nc.sync.dma_start(w2_raw[:], words_of(w2_words))
         l4 = load_list("l4", n4)
-        nc.sync.dma_start(gb_t[:], gb.rearrange("(p t) o -> p (t o)", t=PACK))
         l7 = load_list("l7", n7)
         l5 = load_list("l5", n5)
         l6 = load_list("l6", n6)
@@ -96,178 +103,247 @@ def tile_picked_kqdetwsumtop2_none_po_kernel(
         l9 = load_list("l9", n9)
         l10 = load_list("l10", n10)
 
-        ident = held.tile([P, P], F32, name="ident")
-        make_identity(nc, ident[:])
-
-        def deal(dst, src):
-            nc.vector.tensor_copy(dst[:].rearrange("p (t m) -> p m t", t=PACK), src[:].rearrange("p (m t) -> p m t", t=PACK))
-
-        w1 = held.tile([P, H], I32, name="w1", align_bytes=64)
-        w2 = held.tile([P, H], I32, name="w2", align_bytes=64)
-        ws = held.tile([P, H], U8, name="ws", align_bytes=64)
-
-        def pick(window, lst, dtype, name, tag=None):
-            picked = held.tile([P, S], dtype, name=name, tag=tag or name, align_bytes=64)
-            nc.vector.tensor_copy(picked[:], window.indirect(lst[:]))
+        def pick(source, entries, dtype, name, tag=None):
+            picked = held.tile([P, N], dtype, name=name, tag=tag or name, align_bytes=64)
+            nc.vector.tensor_copy(picked[:], source.indirect(entries[:]))
             return picked
 
-        xa_s = pick(xs[:], l_offs, U8, "xa_s")
-        xb_s = pick(xs[:], l_two, U8, "xb_s")
-        deal(w1, w1_raw)
-        xa_w = pick(xw[:].bitcast(U32), l_offs, U32, "xa_w")
-        deal(ws, ws_raw)
+        def deal(source, dtype, name):
+            dealt = held.tile([P, H], dtype, name=name, align_bytes=64)
+            nc.vector.tensor_copy(
+                dealt[:].bitcast(I32).rearrange("p (t g r) -> p t g r", t=QUARTERS, g=P // RUN),
+                source[:].bitcast(I32).rearrange("p (g t r) -> p t g r", t=QUARTERS, g=P // RUN),
+            )
+            return dealt
 
-        def project(w, first, words, scales, t):
-            bank = psum.tile([P, 512], F32, name="bank")
-            cols = slice(t * P, (t + 1) * P)
+        xa_scale = pick(x_scale[:], l_offs, U8, "xa_scale")
+        xb_scale = pick(x_scale[:], l_two, U8, "xb_scale")
+        xa_word = pick(x_word[:].bitcast(U32), l_offs, U32, "xa_word")
+        w1 = deal(w1_in, I32, "w1")
+        w1_scale = deal(w1_scale_in, U8, "w1_scale")
+
+        gains = held.tile([P, 2 * QUARTERS], F32, name="gains")
+        gain_bank = bank("backs")
+        nc.tensor.transpose(gain_bank[:, 0:P], gain_rows[:], ident[:])
+        nc.scalar.copy(gains[:], gain_bank[:, 0 : 2 * QUARTERS])
+
+        def product(out, lhs_word, lhs_scale, rhs_word, rhs_scale):
             nc.tensor.matmul_mx(
-                bank[:], lhsT=w[:, cols].bitcast(FP8X4), lhsT_scale=ws[first:P, cols],
-                rhs=words[:].bitcast(FP8X4), rhs_scale=scales[:], start=True, stop=True,
-            )
-            return bank
-
-        a_win, ca_win = [], []
-        for t in range(PACK):
-            bank = project(w1, 0, xa_w, xa_s, t)
-            a_t = held.tile([P, 2 * S], F32, name="a%d" % t)
-            ca_t = held.tile([P, 2 * S], F32, name="ca%d" % t)
-            nc.scalar.copy(a_t[:, 0:S], bank[:])
-            nc.scalar.activation(ca_t[:, 0:S], bank[:], ACT.Copy, scale=ga_t[:, t : t + 1])
-            a_win.append(a_t)
-            ca_win.append(ca_t)
-
-        xb_w = pick(xw[:].bitcast(U32), l_two, U32, "xb_w", "ws_raw")
-        deal(w2, w2_raw)
-
-        gb_win, sig, sig7 = [], [], []
-        for t in range(PACK):
-            bank = project(w2, 4, xb_w, xb_s, t)
-            b_t = held.tile([P, 2 * V], F32, name="b%d" % t)
-            gb_b = held.tile([P, 2 * V], F32, name="gbb%d" % t)
-            sig_t = held.tile([P, V], F32, name="sig%d" % t)
-            sig7_t = held.tile([P, V], F32, name="sigg%d" % t)
-            nc.scalar.copy(b_t[:, 0:V], bank[:])
-            nc.scalar.activation(gb_b[:, 0:V], bank[:], ACT.Copy, scale=gb_t[:, t : t + 1])
-            nc.scalar.activation(sig_t[:], bank[:], ACT.Sigmoid)
-            nc.scalar.activation(sig7_t[:], b_t[:].indirect(l7[:]), ACT.Sigmoid)
-            gb_win.append(gb_b)
-            sig.append(sig_t)
-            sig7.append(sig7_t)
-
-        z_banks = [psum.tile([P, 512], F32, name="bank") for jb in range(4)]
-        for t in range(PACK):
-            g1 = work.tile([P, S], F32, name="g1")
-            g3 = work.tile([P, S], F32, name="g3")
-            p12 = work.tile([P, S], F32, name="p12")
-            p34 = work.tile([P, S], F32, name="p34")
-            nc.vector.tensor_scalar(g1[:], a_win[t][:].indirect(l1[:]), 0.75, 0.0, ALU.mult, ALU.add)
-            nc.vector.tensor_scalar(g3[:], a_win[t][:].indirect(l3[:]), -0.75, 0.0, ALU.mult, ALU.add)
-            nc.vector.tensor_tensor(p12[:], ca_win[t][:].indirect(l2[:]), g1[:], ALU.mult)
-            nc.vector.tensor_tensor(p34[:], ca_win[t][:].indirect(l4[:]), g3[:], ALU.mult)
-            for jb in range(4):
-                cols = slice(jb * P, (jb + 1) * P)
-                add_turned(z_banks[jb][:, t * P : (t + 1) * P], [p12[:, cols], p34[:, cols]])
-        z_bf = held.tile([P, S * PACK], BF16, name="z_bf", align_bytes=64)
-        z_pairs = z_bf[:].bitcast(F32).rearrange("p (r m u) -> p r m u", r=PACK, u=2)
-        for h in range(2):
-            back = psum.tile([P, 512], F32, name="bank")
-            for i in range(2):
-                turn_back_pairs(z_banks[2 * h + i], back, i * P)
-            nc.scalar.copy(z_pairs[:, :, 64 * h : 64 * h + 64, :], back[:].rearrange("p (u m r) -> p r m u", u=2, r=PACK))
-        z_w = held.tile([P, S], U32, name="z_w", align_bytes=64)
-        z_s = held.tile([P, S], U8, name="z_s", align_bytes=64)
-
-        def interleave(engine_copy, dst, src):
-            engine_copy(
-                dst[:].rearrange("p (c i t) -> p c t i", i=4, t=PACK),
-                src.rearrange("p t (c i) -> p c t i", i=4),
+                out, lhsT=lhs_word.bitcast(FP8X4), lhsT_scale=lhs_scale,
+                rhs=rhs_word.bitcast(FP8X4), rhs_scale=rhs_scale, start=True, stop=True,
             )
 
-        nc.vector.quantize_mx(z_w[:].bitcast(FP8X4), z_s[:], z_bf[:])
+        def a_windows(t):
+            a_bank = sum_bank(t)
+            product(a_bank[:], w1[:, BLOCKS[t]], w1_scale[:, BLOCKS[t]], xa_word[:], xa_scale[:])
+            a_t = window("a%d" % t)
+            ga_a = window("ga_a%d" % t)
+            nc.scalar.copy(a_t[:, WHOLE], a_bank[:])
+            nc.scalar.activation(ga_a[:, WHOLE], a_bank[:], ACT.Copy, scale=gains[:, t : t + 1])
+            return a_t, ga_a
 
-        z2 = held.tile([P, PACK, V], F32, name="z2")
-        early = held.tile([P, 6 * V], F32, name="early")
-        late = z_bf[:].bitcast(F32)
-        s_win = [held.tile([P, 2 * V], F32, name="s%d" % t) for t in range(PACK)]
+        def b_windows(t):
+            b_bank = bank("backs")
+            product(b_bank[:], w2[:, BLOCKS[t]], w2_scale[:, BLOCKS[t]], xb_word[:], xb_scale[:])
+            b_t = window("b%d" % t)
+            gb_b = window("gb_b%d" % t)
+            sig = held.tile([P, N], F32, name="sig%d" % t)
+            sig7 = held.tile([P, N], F32, name="sig7_%d" % t)
+            nc.scalar.copy(b_t[:, WHOLE], b_bank[:])
+            nc.scalar.activation(gb_b[:, WHOLE], b_bank[:], ACT.Copy, scale=gains[:, QUARTERS + t : QUARTERS + t + 1])
+            nc.scalar.activation(sig[:], b_bank[:], ACT.Sigmoid)
+            nc.scalar.activation(sig7[:], look_up(b_t, l7, WHOLE), ACT.Sigmoid)
+            return gb_b, sig, sig7
 
-        def gated(t, c0, n):
-            pair = early[:, 2 * V * t : 2 * V * (t + 1)] if t < PACK - 1 else late
-            p5_t = pair[:, c0 : c0 + n]
-            p6_t = pair[:, V + c0 : V + c0 + n]
-            nc.vector.tensor_tensor(p5_t, gb_win[t][:].indirect(entries(l5, c0, n)), sig[t][:, c0 : c0 + n], ALU.mult)
-            nc.vector.tensor_tensor(p6_t, gb_win[t][:].indirect(entries(l6, c0, n)), sig7[t][:, c0 : c0 + n], ALU.mult)
-            nc.vector.tensor_tensor(z2[:, t, c0 : c0 + n], p5_t, p6_t, ALU.add)
+        a_win = [a_windows(0)]
+        xb_word = pick(x_word[:].bitcast(U32), l_two, U32, "xb_word", "w1_scale_in")
+        w2 = deal(w2_in, I32, "w2")
+        w2_scale = deal(w2_scale_in, U8, "w2_scale")
+        a_win.extend(a_windows(t) for t in range(1, QUARTERS))
+        b_win = [b_windows(t) for t in range(QUARTERS)]
 
-        for t in range(PACK - 1):
-            gated(t, 0, V)
-        quantised = []
-        for ci, (c0, n) in enumerate(B_PIECES):
-            gated(PACK - 1, c0, n)
-            z2_bf = held.tile([P, n * PACK], BF16, name="z2_bf%d" % ci, align_bytes=64)
-            interleave(nc.vector.tensor_copy if ci == len(B_PIECES) - 1 else nc.scalar.copy, z2_bf, z2[:, :, c0 : c0 + n])
-            z2_w = held.tile([P, n], U32, name="z2_w%d" % ci, align_bytes=64)
-            z2_s = held.tile([P, n], U8, name="z2_s%d" % ci, align_bytes=64)
-            nc.vector.quantize_mx(z2_w[:].bitcast(FP8X4), z2_s[:], z2_bf[:])
-            quantised.append((z2_w, z2_s))
-        last0 = B_PIECES[-1][0]
-        for t in range(PACK):
-            cols = slice(t * P, (t + 1) * P)
-            banks = [psum.tile([P, 512], F32, name="bank") for i in range(2)]
-            for (c0, n), (z2_w, z2_s) in zip(B_PIECES, quantised):
-                nc.tensor.matmul_mx(
-                    banks[c0 // last0][:, c0 : c0 + n], lhsT=z_w[:, cols].bitcast(FP8X4), lhsT_scale=z_s[:, cols],
-                    rhs=z2_w[:].bitcast(FP8X4), rhs_scale=z2_s[:], start=True, stop=True,
+        def add_turned(out, terms):
+            for i, term in enumerate(terms):
+                nc.tensor.matmul(
+                    out, lhsT=term, rhs=ident[:], is_transpose=True, start=(i == 0), stop=(i == len(terms) - 1)
                 )
-            nc.scalar.activation(s_win[t][:, 0:last0], banks[0][:, 0:last0], ACT.Copy, scale=0.03125)
-            nc.scalar.activation(s_win[t][:, last0:V], banks[1][:, last0:V], ACT.Copy, scale=0.03125)
 
-        out_rows = out_0.rearrange("(p t) v -> p t v", t=PACK)
-        out_words = words_of(out_1)
-        out_scales = out_2[0].bitcast(I32)
-        y = held.tile([P, PACK, V], F32, name="y")
-        y_w = held.tile([P, V], I32, name="y_w", align_bytes=64)
-        y_s = held.tile([P, V], U8, name="y_s", align_bytes=64)
-        for t in range(PACK):
-            b1 = work.tile([P, V], F32, name="b1", bufs=G_BUFS)
-            d = work.tile([P, V], F32, name="d")
-            hi = work.tile([P, V], F32, name="hi")
-            ad = work.tile([P, V], F32, name="ad")
-            f = work.tile([P, V], F32, name="f")
-            wv = work.tile([P, V], F32, name="wv")
-            xv = work.tile([P, V], F32, name="xv")
-            pieces = [(0, V)] if t < PACK - 1 else [(0, 256), (256, 256)]
-            for c0, n in pieces:
-                c = slice(c0, c0 + n)
-                nc.vector.tensor_copy(b1[:, c], s_win[t][:].indirect(entries(l8, c0, n)))
-                nc.vector.tensor_tensor(d[:, c], s_win[t][:].indirect(entries(l9, c0, n)), b1[:, c], ALU.subtract)
-                nc.vector.scalar_tensor_tensor(hi[:, c], d[:, c], 0.0, b1[:, c], ALU.max, ALU.add)
-                nc.scalar.activation(ad[:, c], d[:, c], ACT.Abs)
-                nc.vector.tensor_tensor(f[:, c], s_win[t][:].indirect(entries(l10, c0, n)), hi[:, c], ALU.subtract)
-                nc.vector.scalar_tensor_tensor(wv[:, c], f[:, c], -1.0, ad[:, c], ALU.mult, ALU.min)
-                if t < TURNED:
-                    rw = work.tile([P, V], F32, name="rw")
-                    nc.scalar.activation(xv[:], f[:], ACT.Relu, scale=2.0)
-                    nc.scalar.activation(rw[:], wv[:], ACT.Relu)
-                    bank = psum.tile([P, 512], F32, name="bank")
-                    for i in range(V // P):
-                        cols = slice(i * P, (i + 1) * P)
-                        add_turned(bank[:, cols], [hi[:, cols], xv[:, cols], rw[:, cols]])
-                    y_turned = work.tile([P, 512], F32, name="y_turned")
-                    nc.scalar.copy(y_turned[:], bank[:])
-                    back = psum.tile([P, 512], F32, name="bank")
-                    for i in range(V // P):
-                        cols = slice(i * P, (i + 1) * P)
-                        nc.tensor.transpose(back[:, cols], y_turned[:, cols], ident[:])
-                    nc.scalar.copy(y[:, t, :], back[:])
-                else:
-                    nc.vector.scalar_tensor_tensor(xv[:, c], f[:, c], 2.0, wv[:, c], ALU.mult, ALU.max)
-                    nc.vector.tensor_tensor(y[:, t, c], hi[:, c], xv[:, c], ALU.add)
-                nc.sync.dma_start(out_rows[:, t, c], y[:, t, c])
-                if t == PACK - 1:
-                    y_bf = held.tile([P, n * PACK], BF16, name="y_bf%d" % c0, align_bytes=64)
-                    interleave(nc.vector.tensor_copy if c0 else nc.scalar.copy, y_bf, y[:, :, c])
-                    nc.vector.quantize_mx(y_w[:, c].bitcast(FP8X4), y_s[:, c], y_bf[:])
-                    nc.sync.dma_start(out_words[:, c], y_w[:, c])
+        def turn_back_pairs(turned_sums, outs):
+            pairs = work.tile([P, N], BF16, name="pairs", bufs=QUARTERS)
+            nc.scalar.copy(
+                pairs[:].rearrange("j (i p e) -> j i p e", i=2, e=2),
+                turned_sums[:].rearrange("j (i e p) -> j i p e", i=2, e=2),
+            )
+            for i in range(2):
+                nc.tensor.transpose(outs[i], pairs[:].bitcast(F32)[:, BLOCKS[i]], ident[:])
+
+        def weave_pair(copy, woven, u, pair):
+            copy(woven.rearrange("p (c u e) -> p c u e", u=2, e=2)[:, :, u, :], pair.rearrange("p e c -> p c e"))
+
+        def quantise(words, scales, woven):
+            nc.vector.quantize_mx(words.bitcast(FP8X4), scales, woven)
+
+        z_banks = [sum_bank(j) for j in range(len(BLOCKS))]
+        for t, (a_t, ga_a) in enumerate(a_win):
+            a1 = work.tile([P, N], F32, name="a1")
+            a3 = work.tile([P, N], F32, name="a3")
+            a12 = work.tile([P, N], F32, name="a12")
+            a34 = work.tile([P, N], F32, name="a34")
+            nc.vector.tensor_scalar(a1[:], look_up(a_t, l1, WHOLE), 0.75, 0.0, ALU.mult, ALU.add)
+            nc.vector.tensor_scalar(a3[:], look_up(a_t, l3, WHOLE), -0.75, 0.0, ALU.mult, ALU.add)
+            nc.vector.tensor_tensor(a12[:], look_up(ga_a, l2, WHOLE), a1[:], ALU.mult)
+            nc.vector.tensor_tensor(a34[:], look_up(ga_a, l4, WHOLE), a3[:], ALU.mult)
+            for z_bank, cols in zip(z_banks, BLOCKS):
+                add_turned(z_bank[:, BLOCKS[t]], [a12[:, cols], a34[:, cols]])
+
+        b5 = held.tile([P, QUARTERS, N], F32, name="b5")
+        b6 = held.tile([P, QUARTERS, N], F32, name="b6")
+        z2_high = held.tile([P, 2, N], F32, name="z2_high")
+
+        def z2_quarter(t, cols):
+            gb_b, sig, sig7 = b_win[t]
+            nc.vector.tensor_tensor(b5[:, t, cols], look_up(gb_b, l5, cols), sig[:, cols], ALU.mult)
+            nc.vector.tensor_tensor(b6[:, t, cols], look_up(gb_b, l6, cols), sig7[:, cols], ALU.mult)
+            if t >= 2:
+                nc.vector.tensor_tensor(z2_high[:, t - 2, cols], b5[:, t, cols], b6[:, t, cols], ALU.add)
+
+        for t in range(LAST):
+            z2_quarter(t, WHOLE)
+
+        z_woven = held.tile([P, N * QUARTERS], BF16, name="z_woven", align_bytes=64)
+        z_pairs = z_woven[:].bitcast(F32).rearrange("p (t m u) -> p t m u", t=QUARTERS, u=2)
+        for h in range(2):
+            back = bank("backs")
+            for i in range(2):
+                turn_back_pairs(z_banks[2 * h + i], [back[:, BLOCKS[2 * u + i]] for u in range(2)])
+            m = slice(h * HALF // QUARTERS, (h + 1) * HALF // QUARTERS)
+            nc.scalar.copy(z_pairs[:, :, m, :], back[:].rearrange("p (u m t) -> p t m u", u=2, t=QUARTERS))
+
+        z2_banks = [bank("late_sums") for cols in HALVES]
+        for t in range(2):
+            for j, block in enumerate(BLOCKS):
+                add_turned(z2_banks[j // 2][:, BLOCKS[2 * (j % 2) + t]], [b5[:, t, block], b6[:, t, block]])
+        z2_woven = held.tile([P, N * QUARTERS], BF16, name="z2_woven", tag="z2_woven", align_bytes=64)
+        z2_halves = [z2_woven[:, cols.start * QUARTERS : cols.stop * QUARTERS] for cols in HALVES]
+        back = bank("backs")
+        for h in range(2):
+            turn_back_pairs(z2_banks[h], [back[:, BLOCKS[2 * h + i]] for i in range(2)])
+        for woven, cols in zip(z2_halves, HALVES):
+            nc.scalar.copy(woven.bitcast(F32).rearrange("p (c u) -> p c u", u=2)[:, :, 0], back[:, cols])
+
+        z_scale = held.tile([P, N], U8, name="z_scale", align_bytes=64)
+        z_word_first = held.tile([P, P], U32, name="z_word_first", align_bytes=64)
+        quantise(z_word_first[:], z_scale[:, BLOCKS[0]], z_woven[:, 0:N])
+
+        z2_word = held.tile([P, N], U32, name="z2_word", align_bytes=64)
+        z2_scale = held.tile([P, N], U8, name="z2_scale", align_bytes=64)
+        for woven, cols in zip(z2_halves, HALVES):
+            z2_quarter(LAST, cols)
+            weave_pair(nc.vector.tensor_copy, woven, 1, z2_high[:, :, cols])
+            quantise(z2_word[:, cols], z2_scale[:, cols], woven)
+
+        z_word_rest = held.tile([P, N - P], U32, name="z_word_rest", tag="z2_woven", align_bytes=64)
+        quantise(z_word_rest[:, 0:P], z_scale[:, BLOCKS[1]], z_woven[:, N : 2 * N])
+        quantise(z_word_rest[:, P : 3 * P], z_scale[:, HALVES[1]], z_woven[:, 2 * N : 4 * N])
+        z_words = [z_word_first[:]] + [z_word_rest[:, cols] for cols in BLOCKS[:LAST]]
+
+        s_win = [window("s%d" % t, "a%d" % t) for t in range(QUARTERS)]
+
+        def s_quarter(t):
+            banks = [sum_bank(t), bank("backs")]
+            for s_bank, cols in zip(banks, HALVES):
+                product(s_bank[:, cols], z_words[t], z_scale[:, BLOCKS[t]], z2_word[:, cols], z2_scale[:, cols])
+            for s_bank, cols in zip(banks, HALVES):
+                nc.scalar.activation(s_win[t][:, cols], s_bank[:, cols], ACT.Copy, scale=0.0625 / 2)
+
+        out_rows = out_0.rearrange("(p t) v -> p t v", t=QUARTERS)
+        y = held.tile([P, QUARTERS, N], F32, name="y")
+        y_woven = [held.tile([P, HALF * QUARTERS], BF16, name="y_woven%d" % h, align_bytes=64) for h in range(2)]
+        y_word = held.tile([P, N], I32, name="y_word", align_bytes=64)
+        y_scale = held.tile([P, N], U8, name="y_scale", align_bytes=64)
+
+        abs_ds = [held.tile([P, N], F32, name="abs_d%d" % t) for t in range(QUARTERS)]
+
+        def terms_of(t, pieces):
+            abs_d = abs_ds[t]
+            h1 = work.tile([P, N], F32, name="h1")
+            d = work.tile([P, N], F32, name="d")
+            hi = work.tile([P, N], F32, name="hi")
+            f = work.tile([P, N], F32, name="f")
+            w = work.tile([P, N], F32, name="w")
+            for c in pieces:
+                nc.vector.tensor_copy(h1[:, c], look_up(s_win[t], l8, c))
+            for c in pieces:
+                nc.vector.tensor_tensor(d[:, c], look_up(s_win[t], l9, c), h1[:, c], ALU.subtract)
+            for c in pieces:
+                nc.scalar.activation(abs_d[:, c], d[:, c], ACT.Abs)
+            for c in pieces:
+                nc.vector.scalar_tensor_tensor(hi[:, c], d[:, c], 0.0, h1[:, c], ALU.max, ALU.add)
+            for c in pieces:
+                nc.vector.tensor_tensor(f[:, c], look_up(s_win[t], l10, c), hi[:, c], ALU.subtract)
+            for c in pieces:
+                nc.vector.scalar_tensor_tensor(w[:, c], f[:, c], -1.0, abs_d[:, c], ALU.mult, ALU.min)
+            return hi, f, w
+
+        def relu(name, source, scale):
+            out = work.tile([P, N], F32, name=name, bufs=3)
+            nc.scalar.activation(out[:], source[:], ACT.Relu, scale=scale)
+            return out
+
+        def sum_in_psum(t, terms):
+            turned = abs_ds[(t + 2) % QUARTERS]
+            back = bank("backs")
+            banks = [sum_bank(j) for j in range(len(BLOCKS))]
+            for block_bank, cols in zip(banks, BLOCKS):
+                add_turned(block_bank[:, cols], [term[:, cols] for term in terms])
+            for block_bank, cols in zip(banks, BLOCKS):
+                nc.scalar.copy(turned[:, cols], block_bank[:, cols])
+            for cols in BLOCKS:
+                nc.tensor.transpose(back[:, cols], turned[:, cols], ident[:])
+            return back
+
+        def store_rows(t):
+            nc.sync.dma_start(out_rows[:, t, :], y[:, t, :])
+
+        def finish_off_vector(t, hi, f, w):
+            top = relu("top", f, 2.0)
+            mid = relu("mid", w, 1.0)
+            nc.scalar.copy(y[:, t, :], sum_in_psum(t, [hi, top, mid])[:])
+            store_rows(t)
+
+        def finish_from_psum(t, hi, f, w):
+            partial = sum_in_psum(t, [hi, relu("top", f, 2.0)])
+            nc.vector.scalar_tensor_tensor(y[:, t, :], w[:], 0.0, partial[:], ALU.max, ALU.add)
+            store_rows(t)
+
+        def finish_on_vector(t, hi, f, w):
+            rest = work.tile([P, N], F32, name="top", bufs=3)
+            for c in HALVES:
+                nc.vector.scalar_tensor_tensor(rest[:, c], f[:, c], 2.0, w[:, c], ALU.mult, ALU.max)
+            for c in HALVES:
+                nc.vector.tensor_tensor(y[:, t, c], hi[:, c], rest[:, c], ALU.add)
+            store_rows(t)
+
+        s_quarter(0)
+        s_quarter(1)
+        terms = [terms_of(0, [WHOLE]), terms_of(1, [WHOLE])]
+        s_quarter(2)
+        s_quarter(3)
+        finish_off_vector(0, *terms[0])
+        terms.append(terms_of(2, [WHOLE]))
+        finish_off_vector(1, *terms[1])
+        terms.append(terms_of(LAST, HALVES))
+        finish_from_psum(2, *terms[2])
+        for woven, cols in zip(y_woven, HALVES):
+            weave_pair(nc.scalar.copy, woven[:], 0, y[:, 0:2, cols])
+        finish_on_vector(LAST, *terms[LAST])
+
+        for woven, cols in zip(y_woven, HALVES):
+            weave_pair(nc.vector.tensor_copy, woven[:], 1, y[:, 2:4, cols])
+        for woven, cols in zip(y_woven, HALVES):
+            quantise(y_word[:, cols], y_scale[:, cols], woven[:])
+            nc.sync.dma_start(words_of(out_1)[:, cols], y_word[:, cols])
+        scale_rows = out_2[0].bitcast(I32)
         for q in range(4):
-            (nc.sync if q % 2 else nc.scalar).dma_start(
-                out_scales[4 * q : 4 * q + 4, :], y_s[32 * q : 32 * q + 4, :].bitcast(I32))
+            queue = nc.sync if q % 2 else nc.scalar
+            queue.dma_start(scale_rows[4 * q : 4 * q + 4, :], y_scale[32 * q : 32 * q + 4, :].bitcast(I32))

@@ -62,10 +62,6 @@ def tile_picked_kqdetwsumtop2_none_po_kernel(
         ident = held.tile([P, P], F32, name="ident")
         make_identity(nc, ident[:])
 
-        warm = held.tile([P, 2], F32, name="warm")
-        nc.vector.memset(warm[:, 0:1], 0.0)
-        nc.scalar.activation(warm[:, 1:2], warm[:, 0:1], ACT.Sigmoid)
-
         def load_list(name, dram):
             tile = held.tile([P, N // 16], U16, name=name)
             nc.sync.dma_start(tile[:], dram)
@@ -200,15 +196,13 @@ def tile_picked_kqdetwsumtop2_none_po_kernel(
         b6 = held.tile([P, QUARTERS, N], F32, name="b6")
         z2_high = held.tile([P, 2, N], F32, name="z2_high")
 
-        def z2_quarter(t, cols):
+        def z2_terms(t, cols):
             gb_b, sig, sig7 = b_win[t]
             nc.vector.tensor_tensor(b5[:, t, cols], look_up(gb_b, l5, cols), sig[:, cols], ALU.mult)
             nc.vector.tensor_tensor(b6[:, t, cols], look_up(gb_b, l6, cols), sig7[:, cols], ALU.mult)
-            if t >= 2:
-                nc.vector.tensor_tensor(z2_high[:, t - 2, cols], b5[:, t, cols], b6[:, t, cols], ALU.add)
 
         for t in range(LAST):
-            z2_quarter(t, WHOLE)
+            z2_terms(t, WHOLE)
 
         z_woven = held.tile([P, N * QUARTERS], BF16, name="z_woven", align_bytes=64)
         z_pairs = z_woven[:].bitcast(F32).rearrange("p (t m u) -> p t m u", t=QUARTERS, u=2)
@@ -238,7 +232,8 @@ def tile_picked_kqdetwsumtop2_none_po_kernel(
         z2_word = held.tile([P, N], U32, name="z2_word", align_bytes=64)
         z2_scale = held.tile([P, N], U8, name="z2_scale", align_bytes=64)
         for woven, cols in zip(z2_halves, HALVES):
-            z2_quarter(LAST, cols)
+            z2_terms(LAST, cols)
+            nc.vector.tensor_tensor(z2_high[:, :, cols], b5[:, 2:4, cols], b6[:, 2:4, cols], ALU.add)
             weave_pair(nc.vector.tensor_copy, woven, 1, z2_high[:, :, cols])
             quantise(z2_word[:, cols], z2_scale[:, cols], woven)
 

@@ -194,7 +194,6 @@ def tile_picked_kqdetwsumtop2_none_po_kernel(
 
         b5 = held.tile([P, QUARTERS, N], F32, name="b5")
         b6 = held.tile([P, QUARTERS, N], F32, name="b6")
-        z2_high = held.tile([P, 2, N], F32, name="z2_high")
 
         def z2_terms(t, cols):
             gb_b, sig, sig7 = b_win[t]
@@ -233,8 +232,12 @@ def tile_picked_kqdetwsumtop2_none_po_kernel(
         z2_scale = held.tile([P, N], U8, name="z2_scale", align_bytes=64)
         for woven, cols in zip(z2_halves, HALVES):
             z2_terms(LAST, cols)
-            nc.vector.tensor_tensor(z2_high[:, :, cols], b5[:, 2:4, cols], b6[:, 2:4, cols], ALU.add)
-            weave_pair(nc.vector.tensor_copy, woven, 1, z2_high[:, :, cols])
+            nc.vector.tensor_tensor(
+                woven.rearrange("p (c u e) -> p c u e", u=2, e=2)[:, :, 1, :],
+                b5[:, 2:4, cols].rearrange("p e c -> p c e"),
+                b6[:, 2:4, cols].rearrange("p e c -> p c e"),
+                ALU.add,
+            )
             quantise(z2_word[:, cols], z2_scale[:, cols], woven)
 
         z_word_rest = held.tile([P, N - P], U32, name="z_word_rest", tag="z2_woven", align_bytes=64)

from contextlib import ExitStack

import concourse.mybir as mybir
from concourse.masks import make_identity

K, T, S, V, H = 512, 2048, 512, 512, 512
FLOPS = 2 * K * H * S + 2 * K * H * V + 2 * H * S * V

F32 = mybir.dt.float32
BF16 = mybir.dt.bfloat16
I32 = mybir.dt.int32
U32 = mybir.dt.uint32
U16 = mybir.dt.uint16
U8 = mybir.dt.uint8
FP8X4 = mybir.dt.float8_e4m3fn_x4
ALU = mybir.AluOpType
ACT = mybir.ActivationFunctionType

P = 128
QUARTERS = 4
N = 512
RUN = 8
BLOCKS = [slice(c, c + P) for c in range(0, N, P)]
HALF = N // 2
HALVES = [slice(0, HALF), slice(HALF, N)]
WHOLE = slice(0, N)
LAST = QUARTERS - 1


def tile_picked_kqdetwsumtop2_none_po_kernel(
    tc, x_words, x_scales, w1_words, w1_scales, w2_words, w2_scales, ga, gb,
    offs, two, n1, n2, n3, n4, n5, n6, n7, n8, n9, n10, out_0, out_1, out_2,
):
    nc = tc.nc
    with ExitStack() as ctx:
        held = ctx.enter_context(tc.tile_pool(name="held", bufs=1))
        work = ctx.enter_context(tc.tile_pool(name="work", bufs=2))
        psum = ctx.enter_context(tc.psum_pool(name="psum", bufs=2))

        def bank(tag):
            return psum.tile([P, N], F32, name=tag, bufs=4 if tag == "backs" else 2)

        def sum_bank(piece):
            return bank("sums" if piece < 2 else "late_sums")

        def window(name, tag=None):
            return held.tile([P, 2 * N], F32, name=name, tag=tag or name)

        def look_up(tile, entries, cols):
            return tile[:].indirect(entries[:, cols.start // 16 : cols.stop // 16])

        def words_of(dram):
            return dram[0].rearrange("p n t -> p (n t)").bitcast(I32)

        x_scale = held.tile([P, T], U8, name="x_scale", align_bytes=64)
        w1_scale_in = held.tile([P, H], U8, name="w1_scale_in", tag="w1_scale_in", align_bytes=64)
        w2_scale_in = held.tile([P, H], U8, name="w2_scale_in", align_bytes=64)
        gain_rows = held.tile([P, P], F32, name="gain_rows")
        for tile in (x_scale, w1_scale_in, w2_scale_in):
            nc.gpsimd.memset(tile[:].bitcast(I32), 0)
        nc.gpsimd.memset(gain_rows[:], 0.0)
        ident = held.tile([P, P], F32, name="ident")
        make_identity(nc, ident[:])

        def load_list(name, dram):
            tile = held.tile([P, N // 16], U16, name=name)
            nc.sync.dma_start(tile[:], dram)
            return tile

        def load_scales(tile, dram):
            rows = dram[0].bitcast(I32)
            for q in range(4):
                nc.sync.dma_start(tile[32 * q : 32 * q + 4, :].bitcast(I32), rows[4 * q : 4 * q + 4, :])

        x_word = held.tile([P, T], I32, name="x_word", align_bytes=64)
        w1_in = held.tile([P, H], I32, name="w1_in")
        w2_in = held.tile([P, H], I32, name="w2_in")
        load_scales(x_scale, x_scales)
        l_offs = load_list("l_offs", offs)
        l_two = load_list("l_two", two)
        nc.sync.dma_start(x_word[:], words_of(x_words))
        nc.sync.dma_start(w1_in[:], words_of(w1_words))
        load_scales(w1_scale_in, w1_scales)
        l1 = load_list("l1", n1)
        l3 = load_list("l3", n3)
        nc.sync.dma_start(w2_in[:], words_of(w2_words))
        load_scales(w2_scale_in, w2_scales)
        for first, gain in ((0, ga), (QUARTERS, gb)):
            nc.sync.dma_start(
                gain_rows[first : first + QUARTERS, :].rearrange("t (g r) -> t g r", r=RUN),
                gain.rearrange("(g t r) o -> t g (r o)", t=QUARTERS, r=RUN),
            )
        l2 = load_list("l2", n2)
        l4 = load_list("l4", n4)
        l7 = load_list("l7", n7)
        l5 = load_list("l5", n5)
        l6 = load_list("l6", n6)
        l8 = load_list("l8", n8)
        l9 = load_list("l9", n9)
        l10 = load_list("l10", n10)

        def pick(source, entries, dtype, name, tag=None):
            picked = held.tile([P, N], dtype, name=name, tag=tag or name, align_bytes=64)
            nc.vector.tensor_copy(picked[:], source.indirect(entries[:]))
            return picked

        def deal(source, dtype, name):
            dealt = held.tile([P, H], dtype, name=name, align_bytes=64)
            nc.vector.tensor_copy(
                dealt[:].bitcast(I32).rearrange("p (t g r) -> p t g r", t=QUARTERS, g=P // RUN),
                source[:].bitcast(I32).rearrange("p (g t r) -> p t g r", t=QUARTERS, g=P // RUN),
            )
            return dealt

        xa_scale = pick(x_scale[:], l_offs, U8, "xa_scale")
        xb_scale = pick(x_scale[:], l_two, U8, "xb_scale")
        xa_word = pick(x_word[:].bitcast(U32), l_offs, U32, "xa_word")
        w1 = deal(w1_in, I32, "w1")
        w1_scale = deal(w1_scale_in, U8, "w1_scale")

        gains = held.tile([P, 2 * QUARTERS], F32, name="gains")
        gain_bank = bank("backs")
        nc.tensor.transpose(gain_bank[:, 0:P], gain_rows[:], ident[:])
        nc.scalar.copy(gains[:], gain_bank[:, 0 : 2 * QUARTERS])

        def product(out, lhs_word, lhs_scale, rhs_word, rhs_scale):
            nc.tensor.matmul_mx(
                out, lhsT=lhs_word.bitcast(FP8X4), lhsT_scale=lhs_scale,
                rhs=rhs_word.bitcast(FP8X4), rhs_scale=rhs_scale, start=True, stop=True,
            )

        def a_windows(t):
            a_bank = sum_bank(t)
            product(a_bank[:], w1[:, BLOCKS[t]], w1_scale[:, BLOCKS[t]], xa_word[:], xa_scale[:])
            a_t = window("a%d" % t)
            ga_a = window("ga_a%d" % t)
            nc.scalar.copy(a_t[:, WHOLE], a_bank[:])
            nc.scalar.activation(ga_a[:, WHOLE], a_bank[:], ACT.Copy, scale=gains[:, t : t + 1])
            return a_t, ga_a

        def b_windows(t):
            b_bank = bank("backs")
            product(b_bank[:], w2[:, BLOCKS[t]], w2_scale[:, BLOCKS[t]], xb_word[:], xb_scale[:])
            b_t = window("b%d" % t)
            gb_b = window("gb_b%d" % t)
            sig = held.tile([P, N], F32, name="sig%d" % t)
            sig7 = held.tile([P, N], F32, name="sig7_%d" % t)
            nc.scalar.copy(b_t[:, WHOLE], b_bank[:])
            nc.scalar.activation(gb_b[:, WHOLE], b_bank[:], ACT.Copy, scale=gains[:, QUARTERS + t : QUARTERS + t + 1])
            nc.scalar.activation(sig[:], b_bank[:], ACT.Sigmoid)
            nc.scalar.activation(sig7[:], look_up(b_t, l7, WHOLE), ACT.Sigmoid)
            return gb_b, sig, sig7

        a_win = [a_windows(0)]
        xb_word = pick(x_word[:].bitcast(U32), l_two, U32, "xb_word", "w1_scale_in")
        w2 = deal(w2_in, I32, "w2")
        w2_scale = deal(w2_scale_in, U8, "w2_scale")
        a_win.extend(a_windows(t) for t in range(1, QUARTERS))
        b_win = [b_windows(t) for t in range(QUARTERS)]

        def add_turned(out, terms):
            for i, term in enumerate(terms):
                nc.tensor.matmul(
                    out, lhsT=term, rhs=ident[:], is_transpose=True, start=(i == 0), stop=(i == len(terms) - 1)
                )

        def turn_back_pairs(turned_sums, outs):
            pairs = work.tile([P, N], BF16, name="pairs", bufs=QUARTERS)
            nc.scalar.copy(
                pairs[:].rearrange("j (i p e) -> j i p e", i=2, e=2),
                turned_sums[:].rearrange("j (i e p) -> j i p e", i=2, e=2),
            )
            for i in range(2):
                nc.tensor.transpose(outs[i], pairs[:].bitcast(F32)[:, BLOCKS[i]], ident[:])

        def weave_pair(copy, woven, u, pair):
            copy(woven.rearrange("p (c u e) -> p c u e", u=2, e=2)[:, :, u, :], pair.rearrange("p e c -> p c e"))

        def quantise(words, scales, woven):
            nc.vector.quantize_mx(words.bitcast(FP8X4), scales, woven)

        z_banks = [sum_bank(j) for j in range(len(BLOCKS))]
        for t, (a_t, ga_a) in enumerate(a_win):
            a1 = work.tile([P, N], F32, name="a1")
            a3 = work.tile([P, N], F32, name="a3")
            a12 = work.tile([P, N], F32, name="a12")
            a34 = work.tile([P, N], F32, name="a34")
            nc.vector.tensor_scalar(a1[:], look_up(a_t, l1, WHOLE), 0.75, 0.0, ALU.mult, ALU.add)
            nc.vector.tensor_scalar(a3[:], look_up(a_t, l3, WHOLE), -0.75, 0.0, ALU.mult, ALU.add)
            nc.vector.tensor_tensor(a12[:], look_up(ga_a, l2, WHOLE), a1[:], ALU.mult)
            nc.vector.tensor_tensor(a34[:], look_up(ga_a, l4, WHOLE), a3[:], ALU.mult)
            for z_bank, cols in zip(z_banks, BLOCKS):
                add_turned(z_bank[:, BLOCKS[t]], [a12[:, cols], a34[:, cols]])

        b5 = held.tile([P, QUARTERS, N], F32, name="b5")
        b6 = held.tile([P, QUARTERS, N], F32, name="b6")

        def z2_terms(t, cols):
            gb_b, sig, sig7 = b_win[t]
            nc.vector.tensor_tensor(b5[:, t, cols], look_up(gb_b, l5, cols), sig[:, cols], ALU.mult)
            nc.vector.tensor_tensor(b6[:, t, cols], look_up(gb_b, l6, cols), sig7[:, cols], ALU.mult)

        for t in range(LAST):
            z2_terms(t, WHOLE)

        z_woven = held.tile([P, N * QUARTERS], BF16, name="z_woven", align_bytes=64)
        z_pairs = z_woven[:].bitcast(F32).rearrange("p (t m u) -> p t m u", t=QUARTERS, u=2)
        for h in range(2):
            back = bank("backs")
            for i in range(2):
                turn_back_pairs(z_banks[2 * h + i], [back[:, BLOCKS[2 * u + i]] for u in range(2)])
            m = slice(h * HALF // QUARTERS, (h + 1) * HALF // QUARTERS)
            nc.scalar.copy(z_pairs[:, :, m, :], back[:].rearrange("p (u m t) -> p t m u", u=2, t=QUARTERS))

        z2_banks = [bank("late_sums") for cols in HALVES]
        for t in range(2):
            for j, block in enumerate(BLOCKS):
                add_turned(z2_banks[j // 2][:, BLOCKS[2 * (j % 2) + t]], [b5[:, t, block], b6[:, t, block]])
        z2_woven = held.tile([P, N * QUARTERS], BF16, name="z2_woven", tag="z2_woven", align_bytes=64)
        z2_halves = [z2_woven[:, cols.start * QUARTERS : cols.stop * QUARTERS] for cols in HALVES]
        back = bank("backs")
        for h in range(2):
            turn_back_pairs(z2_banks[h], [back[:, BLOCKS[2 * h + i]] for i in range(2)])
        for woven, cols in zip(z2_halves, HALVES):
            nc.scalar.copy(woven.bitcast(F32).rearrange("p (c u) -> p c u", u=2)[:, :, 0], back[:, cols])

        z_scale = held.tile([P, N], U8, name="z_scale", align_bytes=64)
        z_word_first = held.tile([P, P], U32, name="z_word_first", align_bytes=64)
        quantise(z_word_first[:], z_scale[:, BLOCKS[0]], z_woven[:, 0:N])

        z2_word = held.tile([P, N], U32, name="z2_word", align_bytes=64)
        z2_scale = held.tile([P, N], U8, name="z2_scale", align_bytes=64)
        for woven, cols in zip(z2_halves, HALVES):
            z2_terms(LAST, cols)
            nc.vector.tensor_tensor(
                woven.rearrange("p (c u e) -> p c u e", u=2, e=2)[:, :, 1, :],
                b5[:, 2:4, cols].rearrange("p e c -> p c e"),
                b6[:, 2:4, cols].rearrange("p e c -> p c e"),
                ALU.add,
            )
            quantise(z2_word[:, cols], z2_scale[:, cols], woven)

        z_word_rest = held.tile([P, N - P], U32, name="z_word_rest", tag="z2_woven", align_bytes=64)
        quantise(z_word_rest[:, 0:P], z_scale[:, BLOCKS[1]], z_woven[:, N : 2 * N])
        quantise(z_word_rest[:, P : 3 * P], z_scale[:, HALVES[1]], z_woven[:, 2 * N : 4 * N])
        z_words = [z_word_first[:]] + [z_word_rest[:, cols] for cols in BLOCKS[:LAST]]

        s_win = [window("s%d" % t, "a%d" % t) for t in range(QUARTERS)]

        def s_quarter(t):
            banks = [sum_bank(t), bank("backs")]
            for s_bank, cols in zip(banks, HALVES):
                product(s_bank[:, cols], z_words[t], z_scale[:, BLOCKS[t]], z2_word[:, cols], z2_scale[:, cols])
            for s_bank, cols in zip(banks, HALVES):
                nc.scalar.activation(s_win[t][:, cols], s_bank[:, cols], ACT.Copy, scale=0.0625 / 2)

        out_rows = out_0.rearrange("(p t) v -> p t v", t=QUARTERS)
        y = held.tile([P, QUARTERS, N], F32, name="y")
        y_woven = [held.tile([P, HALF * QUARTERS], BF16, name="y_woven%d" % h, align_bytes=64) for h in range(2)]
        y_word = held.tile([P, N], I32, name="y_word", align_bytes=64)
        y_scale = held.tile([P, N], U8, name="y_scale", align_bytes=64)

        abs_ds = [held.tile([P, N], F32, name="abs_d%d" % t) for t in range(QUARTERS)]

        def terms_of(t, pieces):
            abs_d = abs_ds[t]
            h1 = work.tile([P, N], F32, name="h1")
            d = work.tile([P, N], F32, name="d")
            hi = work.tile([P, N], F32, name="hi")
            f = work.tile([P, N], F32, name="f")
            w = work.tile([P, N], F32, name="w")
            for c in pieces:
                nc.vector.tensor_copy(h1[:, c], look_up(s_win[t], l8, c))
            for c in pieces:
                nc.vector.tensor_tensor(d[:, c], look_up(s_win[t], l9, c), h1[:, c], ALU.subtract)
            for c in pieces:
                nc.scalar.activation(abs_d[:, c], d[:, c], ACT.Abs)
            for c in pieces:
                nc.vector.scalar_tensor_tensor(hi[:, c], d[:, c], 0.0, h1[:, c], ALU.max, ALU.add)
            for c in pieces:
                nc.vector.tensor_tensor(f[:, c], look_up(s_win[t], l10, c), hi[:, c], ALU.subtract)
            for c in pieces:
                nc.vector.scalar_tensor_tensor(w[:, c], f[:, c], -1.0, abs_d[:, c], ALU.mult, ALU.min)
            return hi, f, w

        def relu(name, source, scale):
            out = work.tile([P, N], F32, name=name, bufs=3)
            nc.scalar.activation(out[:], source[:], ACT.Relu, scale=scale)
            return out

        def sum_in_psum(t, terms):
            turned = abs_ds[(t + 2) % QUARTERS]
            back = bank("backs")
            banks = [sum_bank(j) for j in range(len(BLOCKS))]
            for block_bank, cols in zip(banks, BLOCKS):
                add_turned(block_bank[:, cols], [term[:, cols] for term in terms])
            for block_bank, cols in zip(banks, BLOCKS):
                nc.scalar.copy(turned[:, cols], block_bank[:, cols])
            for cols in BLOCKS:
                nc.tensor.transpose(back[:, cols], turned[:, cols], ident[:])
            return back

        def store_rows(t):
            nc.sync.dma_start(out_rows[:, t, :], y[:, t, :])

        def finish_off_vector(t, hi, f, w):
            top = relu("top", f, 2.0)
            mid = relu("mid", w, 1.0)
            nc.scalar.copy(y[:, t, :], sum_in_psum(t, [hi, top, mid])[:])
            store_rows(t)

        def finish_from_psum(t, hi, f, w):
            partial = sum_in_psum(t, [hi, relu("top", f, 2.0)])
            nc.vector.scalar_tensor_tensor(y[:, t, :], w[:], 0.0, partial[:], ALU.max, ALU.add)
            store_rows(t)

        def finish_on_vector(t, hi, f, w):
            rest = work.tile([P, N], F32, name="top", bufs=3)
            for c in HALVES:
                nc.vector.scalar_tensor_tensor(rest[:, c], f[:, c], 2.0, w[:, c], ALU.mult, ALU.max)
            for c in HALVES:
                nc.vector.tensor_tensor(y[:, t, c], hi[:, c], rest[:, c], ALU.add)
            store_rows(t)

        s_quarter(0)
        s_quarter(1)
        terms = [terms_of(0, [WHOLE]), terms_of(1, [WHOLE])]
        s_quarter(2)
        s_quarter(3)
        finish_off_vector(0, *terms[0])
        terms.append(terms_of(2, [WHOLE]))
        finish_off_vector(1, *terms[1])
        terms.append(terms_of(LAST, HALVES))
        finish_from_psum(2, *terms[2])
        for woven, cols in zip(y_woven, HALVES):
            weave_pair(nc.scalar.copy, woven[:], 0, y[:, 0:2, cols])
        finish_on_vector(LAST, *terms[LAST])

        for woven, cols in zip(y_woven, HALVES):
            weave_pair(nc.vector.tensor_copy, woven[:], 1, y[:, 2:4, cols])
        for woven, cols in zip(y_woven, HALVES):
            quantise(y_word[:, cols], y_scale[:, cols], woven[:])
            nc.sync.dma_start(words_of(out_1)[:, cols], y_word[:, cols])
        scale_rows = out_2[0].bitcast(I32)
        for q in range(4):
            queue = nc.sync if q % 2 else nc.scalar
            queue.dma_start(scale_rows[4 * q : 4 * q + 4, :], y_scale[32 * q : 32 * q + 4, :].bitcast(I32))
